import numpy as np, ml_dtypes
CORES = [5,13,29,37,53,69,77,101,133,141,157,165,181,197,205,229]
N = 16
import mx_ref
NC = 256
BF = ml_dtypes.bfloat16
def setup_inputs(rng):
    def f(*shape):
        return mx_ref.flush((rng.standard_normal(shape, dtype=np.float32) * np.exp2(rng.integers(-2, 3, shape[:-1] + (1,)))).astype(BF))
    return {"c": f(N, 128, 512), "x": f(N, 128, 4 * NC)}
def setup_inputs_blocks(rng):
    d = setup_inputs(rng)
    for k in ("c", "x"): d[k] = mx_ref.spread(d[k], rng, 2)
    return d
def setup_inputs_wide(rng):
    d = setup_inputs(rng)
    for k in ("c", "x"): d[k] = mx_ref.flush((d[k].astype(np.float32) * np.exp2(rng.integers(-8, 9, (N, 1, 1))).astype(np.float32)).astype(BF))
    return d
def reference(c, x):
    QC = [mx_ref.quantize(c[k]) for k in range(N)]; QX = [mx_ref.quantize(x[j]) for j in range(N)]
    y = np.zeros((N, 128, NC), np.float32)
    for r in range(N):
        for j in range(N):
            p = mx_ref.matmul(QC[(r - j) % N], QX[j])
            y[r] = p if j == 0 else y[r] + p
    return {"y": y}

@@ -1,0 +1,169 @@
+from concourse.bass import DstId, RemoteDMATransfer
+from concourse.mybir import dt
+
+N = 16
+WORLD = 256
+CW, XW = 128, 256
+W = CW + XW
+
+SCRATCH = {
+    "Q": ("sbuf", [128, N * W], "float8_e4m3fn_x4"),
+    "S": ("sbuf", [128, N * W], "uint8"),
+    "cin": ("sbuf", [128, 4 * CW], "bfloat16"),
+    "xin": ("sbuf", [128, 4 * XW], "bfloat16"),
+    "acc": ("psum", [128, 512], "float32"),
+    "yout": ("sbuf", [128, XW], "float32"),
+}
+SEMAPHORES = (["aq%d" % s for s in range(N)] + ["as%d" % s for s in range(N)]
+              + ["ldc", "ldx", "qz", "sent", "mm", "cp", "st"])
+
+T_PLANE_ON, T_CODES_ON = 0.17, 0.33
+T_CODES_OFF, T_BOTH_OFF = 0.67, 1.0
+T_HOP = 1.0
+T_NEAR = 0.4
+
+_CACHE = {}
+
+
+def _bits(mask):
+    return bin(mask).count("1")
+
+
+def _plan(cores, topo):
+    if "p" in _CACHE:
+        return _CACHE["p"]
+    ops, when, arrive, inload = {}, {}, {}, {}
+
+    def add(core, s, dsts):
+        mask = topo.mask(core, dsts[0])
+        for d in dsts:
+            mask &= topo.mask(core, d)
+        for kind in ("S", "Q"):
+            ops.setdefault(core, []).append((kind, s, dsts, mask))
+            for d in dsts:
+                arrive[(d, kind, s)] = _bits(mask)
+
+    for s, root in enumerate(cores):
+        chipmates = [c for c in range(WORLD) if c != root and topo.host(c) == topo.host(root) and topo.chip(c) == topo.chip(root)]
+        dests = [(r, d) for r, d in enumerate(cores) if d != root]
+
+        def by_turns(cs):
+            a = [c for c in cs if topo.die(c) == topo.die(root)]
+            b = [c for c in cs if topo.die(c) != topo.die(root)]
+            out = []
+            while a or b:
+                if a:
+                    out.append(a.pop(0))
+                if b:
+                    out.append(b.pop(0))
+            return out
+
+        free_all = by_turns([h for h in chipmates if all(topo.may_write(h, d) for _, d in dests)])
+        helpers = free_all + by_turns([h for h in chipmates if h not in free_all])
+        k = len(helpers)
+        free = {h: k * T_PLANE_ON + (i + 1) * T_CODES_ON + T_HOP for i, h in enumerate(helpers)}
+        step = {h: T_CODES_OFF for h in helpers}
+        free[root], step[root] = k * (T_PLANE_ON + T_CODES_ON), T_BOTH_OFF
+        barred = [x for x in dests if not topo.may_write(root, x[1])]
+        open_ = [x for x in dests if topo.may_write(root, x[1])]
+        slots = []
+        for group, cand in ((barred, free_all), (open_, helpers + [root])):
+            for _ in group:
+                c = min(cand, key=lambda c: free[c] + step[c])
+                free[c] += step[c]
+                slots.append((free[c], c))
+        slots.sort()
+        order = sorted(dests, key=lambda x: (min((2 * s - x[0]) % N, (x[0] - 2 * s) % N), (x[0] - s) % N))
+        left = len(barred)
+        give = {}
+        for r, d in order:
+            is_barred = not topo.may_write(root, d)
+            ok = [sl for sl in slots if sl[1] in free_all or not is_barred]
+            if not is_barred and sum(1 for sl in slots if sl[1] in free_all) <= left:
+                ok = [sl for sl in ok if sl[1] not in free_all]
+            near = [sl for sl in ok if sl[0] <= ok[0][0] + T_NEAR]
+            sl = min(near, key=lambda sl: (inload.get((d, topo.die(sl[1])), 0), sl[0]))
+            slots.remove(sl)
+            left -= 1 if is_barred else 0
+            key = (d, topo.die(sl[1]))
+            inload[key] = inload.get(key, 0) + 1
+            give.setdefault(sl[1], []).append((sl[0], d))
+            when[(s, r)] = sl[0]
+        used = [h for h in helpers if h in give]
+        add(root, s, used)
+        for c in used + [root]:
+            if c in give:
+                add(c, s, [d for _, d in sorted(give[c])])
+    _CACHE["p"] = (ops, when, arrive)
+    return _CACHE["p"]
+
+
+def rank_program(g, core, T, topo):
+    cores = list(T.cores)
+    ops, when, arrive = _plan(cores, topo)
+    rank = T.rank_of(core)
+    mine = ops.get(core, [])
+    if rank is None and not mine:
+        return
+    sem = T.sem
+
+    if rank is not None:
+        b = rank * W
+        g.sync.dma_start(T.cin[:], T.c[:]).then_inc(sem.ldc, 16)
+        g.scalar.dma_start(T.xin[:], T.x[:]).then_inc(sem.ldx, 16)
+        g.vector.wait_ge(sem.ldc, 16)
+        g.vector.quantize_mx(T.Q[:, b:b + CW], T.S[:, b:b + CW], T.cin[:]).then_inc(sem.qz, 1)
+        g.vector.wait_ge(sem.ldx, 16)
+        g.vector.quantize_mx(T.Q[:, b + CW:b + W], T.S[:, b + CW:b + W], T.xin[:]).then_inc(sem.qz, 1)
+        g.wait_ge(sem.qz, 2)
+
+    sent = 0
+    for kind, s, dsts, mask in mine:
+        name = ("aq%d" if kind == "Q" else "as%d") % s
+        if cores[s] != core:
+            g.wait_ge(sem[name], arrive[(core, kind, s)])
+
+        def view():
+            if kind == "Q":
+                return T.Q[:, s * W:(s + 1) * W].bitcast(dt.uint8)
+            return T.S[:, s * W:(s + 1) * W]
+
+        ids = []
+        for d in dsts:
+            rid, pid = topo.addr(d, core)
+            ids.append(DstId(rid=rid, pnc=pid))
+        g.remote_dma_fused([RemoteDMATransfer(dst_ids=ids, dma_engine_mask=mask, remote_sem=sem[name],
+                                              srcs=[view()], dsts=[view() for _ in dsts])], local_sem=sem.sent)
+        sent += _bits(mask)
+
+    if rank is not None:
+        def ready(j):
+            return max(when.get((j, rank), 0.0), when.get(((rank - j) % N, rank), 0.0))
+
+        order = sorted(range(N), key=lambda j: (ready(j), j))
+        seen = set()
+        for i, j in enumerate(order):
+            kk = (rank - j) % N
+            for t in (j, kk):
+                if t in seen:
+                    continue
+                seen.add(t)
+                if t == rank:
+                    g.tensor.wait_ge(sem.qz, 2)
+                else:
+                    g.tensor.wait_ge(sem["as%d" % t], arrive[(core, "S", t)])
+                    g.tensor.wait_ge(sem["aq%d" % t], arrive[(core, "Q", t)])
+            mmx = g.tensor.matmul_mx(T.acc[:, 0:XW],
+                                     T.Q[:, kk * W:kk * W + CW], T.S[:, kk * W:kk * W + CW],
+                                     T.Q[:, j * W + CW:(j + 1) * W], T.S[:, j * W + CW:(j + 1) * W],
+                                     i == 0, i == N - 1)
+            if i == N - 1:
+                mmx.then_inc(sem.mm, 1)
+        g.vector.wait_ge(sem.mm, 1)
+        g.vector.tensor_copy(T.yout[:], T.acc[:, 0:XW]).then_inc(sem.cp, 1)
+        g.sync.wait_ge(sem.cp, 1)
+        g.sync.dma_start(T.y[:], T.yout[:]).then_inc(sem.st, 16)
+        g.sync.wait_ge(sem.st, 16)
+
+    if sent:
+        g.wait_ge(sem.sent, sent)

@@ -17,10 +17,12 @@ SCRATCH = {
 SEMAPHORES = (["aq%d" % s for s in range(N)] + ["as%d" % s for s in range(N)]
               + ["ldc", "ldx", "qz", "sent", "mm", "cp", "st"])
 
-T_PLANE_ON, T_CODES_ON = 0.17, 0.33
-T_CODES_OFF, T_BOTH_OFF = 0.67, 1.0
-T_HOP = 1.0
-T_NEAR = 0.4
+TPO, TCO = 0.17, 0.33
+TPF, TCF = 0.33, 0.67
+THOP = 1.0
+TNEAR = 0.4
+SW_SHARE = (3 * (N - 1)) // 5
+CAP = 1
 
 _CACHE = {}
 
@@ -32,19 +34,43 @@ def _bits(mask):
 def _plan(cores, topo):
     if "p" in _CACHE:
         return _CACHE["p"]
-    ops, when, arrive, inload = {}, {}, {}, {}
+    raw, when, arrive, inload, gwload, gwjobs = {}, {}, {}, {}, {}, {}
 
-    def add(core, s, dsts):
-        mask = topo.mask(core, dsts[0])
-        for d in dsts:
-            mask &= topo.mask(core, d)
-        for kind in ("S", "Q"):
-            ops.setdefault(core, []).append((kind, s, dsts, mask))
-            for d in dsts:
-                arrive[(d, kind, s)] = _bits(mask)
+    def place(c):
+        return (topo.host(c), topo.chip(c))
+
+    def add(t, core, kind, s, dsts):
+        off = [d for d in dsts if place(d) != place(core)]
+        on = [d for d in dsts if place(d) == place(core)]
+        groups, taken = [], 0
+        if off:
+            m = topo.mask(core, off[0])
+            for d in off:
+                m &= topo.mask(core, d)
+            groups.append((m, off))
+            taken = m
+        if on:
+            groups.append((topo.mask(core, on[0]) & ~taken, on))
+        for m, ds in groups:
+            for d in ds:
+                arrive[(d, kind, s)] = _bits(m)
+        raw.setdefault(core, []).append((t, kind, s, groups))
+
+    def has_mate(c):
+        return any(topo.mates(c, d) for d in cores)
+
+    straight = set()
+    for r, d in enumerate(cores):
+        same = [s for s, c in enumerate(cores) if c != d and topo.may_write(c, d)]
+        cross = [s for s, c in enumerate(cores) if c != d and not topo.may_write(c, d) and not topo.mates(c, d)]
+        idle = [s for s in cross if not has_mate(cores[s])]
+        pref = idle + [s for s in cross if s not in idle]
+        q = max(0, SW_SHARE - len(same))
+        for i in range(q):
+            straight.add((pref[(i + r) % len(idle)] if q <= len(idle) else pref[i], r))
 
     for s, root in enumerate(cores):
-        chipmates = [c for c in range(WORLD) if c != root and topo.host(c) == topo.host(root) and topo.chip(c) == topo.chip(root)]
+        chipmates = [c for c in range(WORLD) if c != root and place(c) == place(root)]
         dests = [(r, d) for r, d in enumerate(cores) if d != root]
 
         def by_turns(cs):
@@ -58,42 +84,92 @@ def _plan(cores, topo):
                     out.append(b.pop(0))
             return out
 
+        def pi(r):
+            return min((2 * s - r) % N, (r - 2 * s) % N)
+
         free_all = by_turns([h for h in chipmates if all(topo.may_write(h, d) for _, d in dests)])
         helpers = free_all + by_turns([h for h in chipmates if h not in free_all])
+        idx = {h: i for i, h in enumerate(helpers)}
         k = len(helpers)
-        free = {h: k * T_PLANE_ON + (i + 1) * T_CODES_ON + T_HOP for i, h in enumerate(helpers)}
-        step = {h: T_CODES_OFF for h in helpers}
-        free[root], step[root] = k * (T_PLANE_ON + T_CODES_ON), T_BOTH_OFF
-        barred = [x for x in dests if not topo.may_write(root, x[1])]
-        open_ = [x for x in dests if topo.may_write(root, x[1])]
+
+        targets, covered = [], set()
+        for r, d in dests:
+            if topo.may_write(root, d):
+                continue
+            covered.add(r)
+            if topo.mates(root, d) or (s, r) in straight:
+                targets.append(("X", [(r, d)], [], place(d)))
+            else:
+                gws = [c for c in range(WORLD) if topo.mates(c, d) and topo.may_write(c, d)]
+                local = [x for x in dests if place(x[1]) == place(gws[0])]
+                covered.update(x[0] for x in local)
+                targets.append(("G", [(r, d)] + local, gws, place(gws[0])))
+        for r, d in dests:
+            if r not in covered:
+                targets.append(("R", [(r, d)], [], place(d)))
+
+        free = {h: k * TPO + (i + 1) * TCO + THOP for i, h in enumerate(helpers)}
+        step = {h: TCF for h in helpers}
+        free[root], step[root] = k * (TPO + TCO), TPF + TCF
+        count = {}
+        busy = has_mate(root)
+        n_x = sum(1 for t in targets if t[0] == "X")
         slots = []
-        for group, cand in ((barred, free_all), (open_, helpers + [root])):
-            for _ in group:
-                c = min(cand, key=lambda c: free[c] + step[c])
+        for n, cand in ((n_x, free_all), (len(targets) - n_x, helpers + [root])):
+            for _ in range(n):
+                cc = [c for c in cand if not (busy and c in free_all and count.get(c, 0) >= CAP)] or cand
+                c = min(cc, key=lambda c: free[c] + step[c])
                 free[c] += step[c]
+                count[c] = count.get(c, 0) + 1
                 slots.append((free[c], c))
         slots.sort()
-        order = sorted(dests, key=lambda x: (min((2 * s - x[0]) % N, (x[0] - 2 * s) % N), (x[0] - s) % N))
-        left = len(barred)
-        give = {}
-        for r, d in order:
-            is_barred = not topo.may_write(root, d)
-            ok = [sl for sl in slots if sl[1] in free_all or not is_barred]
-            if not is_barred and sum(1 for sl in slots if sl[1] in free_all) <= left:
+
+        left, give = n_x, {}
+        for t in sorted(targets, key=lambda t: (t[0] != "G", min(pi(r) for r, _ in t[1]))):
+            is_x = t[0] == "X"
+            ok = [sl for sl in slots if sl[1] in free_all or not is_x]
+            if not is_x and sum(1 for sl in slots if sl[1] in free_all) <= left:
                 ok = [sl for sl in ok if sl[1] not in free_all]
-            near = [sl for sl in ok if sl[0] <= ok[0][0] + T_NEAR]
-            sl = min(near, key=lambda sl: (inload.get((d, topo.die(sl[1])), 0), sl[0]))
+            near = [sl for sl in ok if sl[0] <= ok[0][0] + TNEAR]
+            sl = min(near, key=lambda sl: (inload.get((t[3], topo.die(sl[1])), 0), sl[0]))
             slots.remove(sl)
-            left -= 1 if is_barred else 0
-            key = (d, topo.die(sl[1]))
+            left -= 1 if is_x else 0
+            key = (t[3], topo.die(sl[1]))
             inload[key] = inload.get(key, 0) + 1
-            give.setdefault(sl[1], []).append((sl[0], d))
-            when[(s, r)] = sl[0]
+            give.setdefault(sl[1], []).append((sl[0], t))
+
         used = [h for h in helpers if h in give]
-        add(root, s, used)
+        add(0.0, root, "S", s, used)
+        add(0.01, root, "Q", s, used)
         for c in used + [root]:
-            if c in give:
-                add(c, s, [d for _, d in sorted(give[c])])
+            if c not in give:
+                continue
+            ts0 = TPO * (idx[c] + 1) if c != root else k * (TPO + TCO)
+            tq0 = k * TPO + (idx[c] + 1) * TCO if c != root else k * (TPO + TCO) + 0.01
+            hop = THOP if c != root else 0.0
+            land = []
+            for pos, (tq, t) in enumerate(sorted(give[c], key=lambda x: x[0])):
+                if t[0] == "G":
+                    gw = min([x for x in t[2] if topo.die(x) == topo.die(c)], key=lambda x: gwload.get(x, 0))
+                    gwload[gw] = gwload.get(gw, 0) + 1
+                    land.append(gw)
+                    gwjobs.setdefault(gw, []).append((tq, ts0 + hop + TPF * (pos + 1), s, t[1]))
+                else:
+                    land.append(t[1][0][1])
+                    when[(s, t[1][0][0])] = tq
+            add(ts0, c, "S", s, land)
+            add(tq0, c, "Q", s, land)
+
+    for gw, jobs in gwjobs.items():
+        f = 0.0
+        for tq, ts, s, fin in sorted(jobs, key=lambda x: x[0]):
+            add(ts, gw, "S", s, [d for _, d in fin])
+            add(tq, gw, "Q", s, [d for _, d in fin])
+            t = max(f, tq + THOP) + TCF
+            f = t + TPF
+            for r, _ in fin:
+                when[(s, r)] = t
+    ops = {c: [x[1:] for x in sorted(l, key=lambda x: x[0])] for c, l in raw.items()}
     _CACHE["p"] = (ops, when, arrive)
     return _CACHE["p"]
 
@@ -118,7 +194,7 @@ def rank_program(g, core, T, topo):
         g.wait_ge(sem.qz, 2)
 
     sent = 0
-    for kind, s, dsts, mask in mine:
+    for kind, s, groups in mine:
         name = ("aq%d" if kind == "Q" else "as%d") % s
         if cores[s] != core:
             g.wait_ge(sem[name], arrive[(core, kind, s)])
@@ -128,13 +204,16 @@ def rank_program(g, core, T, topo):
                 return T.Q[:, s * W:(s + 1) * W].bitcast(dt.uint8)
             return T.S[:, s * W:(s + 1) * W]
 
-        ids = []
-        for d in dsts:
-            rid, pid = topo.addr(d, core)
-            ids.append(DstId(rid=rid, pnc=pid))
-        g.remote_dma_fused([RemoteDMATransfer(dst_ids=ids, dma_engine_mask=mask, remote_sem=sem[name],
-                                              srcs=[view()], dsts=[view() for _ in dsts])], local_sem=sem.sent)
-        sent += _bits(mask)
+        transfers = []
+        for mask, dsts in groups:
+            ids = []
+            for d in dsts:
+                rid, pid = topo.addr(d, core)
+                ids.append(DstId(rid=rid, pnc=pid))
+            transfers.append(RemoteDMATransfer(dst_ids=ids, dma_engine_mask=mask, remote_sem=sem[name],
+                                               srcs=[view()], dsts=[view() for _ in dsts]))
+            sent += _bits(mask)
+        g.remote_dma_fused(transfers, local_sem=sem.sent)
 
     if rank is not None:
         def ready(j):

@@ -5,6 +5,9 @@ N = 16
 WORLD = 256
 CW, XW = 128, 256
 W = CW + XW
+PIECES = (("Q", 0, CW), ("Q", CW, CW + XW // 2), ("Q", CW + XW // 2, W), ("S", 0, W))
+PLANE = 3
+MAXCROSS = 5
 
 SCRATCH = {
     "Q": ("sbuf", [128, N * W], "float8_e4m3fn_x4"),
@@ -14,15 +17,7 @@ SCRATCH = {
     "acc": ("psum", [128, 512], "float32"),
     "yout": ("sbuf", [128, XW], "float32"),
 }
-SEMAPHORES = (["aq%d" % s for s in range(N)] + ["as%d" % s for s in range(N)]
-              + ["ldc", "ldx", "qz", "sent", "mm", "cp", "st"])
-
-TPO, TCO = 0.17, 0.33
-TPF, TCF = 0.33, 0.67
-THOP = 1.0
-TNEAR = 0.4
-SW_SHARE = (3 * (N - 1)) // 5
-CAP = 1
+SEMAPHORES = ["a%d" % s for s in range(N)] + ["ldc", "ldx", "qz", "sent", "mm", "cp", "st"]
 
 _CACHE = {}
 
@@ -34,142 +29,153 @@ def _bits(mask):
 def _plan(cores, topo):
     if "p" in _CACHE:
         return _CACHE["p"]
-    raw, when, arrive, inload, gwload, gwjobs = {}, {}, {}, {}, {}, {}
+    raw, when, arrive, gwjobs = {}, {}, {}, {}
 
     def place(c):
         return (topo.host(c), topo.chip(c))
 
-    def add(t, core, kind, s, dsts):
-        off = [d for d in dsts if place(d) != place(core)]
-        on = [d for d in dsts if place(d) == place(core)]
-        groups, taken = [], 0
-        if off:
-            m = topo.mask(core, off[0])
-            for d in off:
-                m &= topo.mask(core, d)
-            groups.append((m, off))
-            taken = m
-        if on:
-            groups.append((topo.mask(core, on[0]) & ~taken, on))
-        for m, ds in groups:
+    def on_chip(c):
+        return [x for x in range(WORLD) if place(x) == place(c)]
+
+    def plane_of(c):
+        return 0 if place(c) == place(cores[0]) or topo.same_plane(c, cores[0]) else 1
+
+    def call(t, core, s, transfers):
+        for _, m, ds in transfers:
             for d in ds:
-                arrive[(d, kind, s)] = _bits(m)
-        raw.setdefault(core, []).append((t, kind, s, groups))
+                arrive[(d, s)] = arrive.get((d, s), 0) + _bits(m)
+        raw.setdefault(core, []).append((t, s, transfers))
 
-    def has_mate(c):
-        return any(topo.mates(c, d) for d in cores)
+    def off_mask(c, ds):
+        m = topo.mask(c, ds[0])
+        for d in ds:
+            m &= topo.mask(c, d)
+        return m
 
-    straight = set()
-    for r, d in enumerate(cores):
-        same = [s for s, c in enumerate(cores) if c != d and topo.may_write(c, d)]
-        cross = [s for s, c in enumerate(cores) if c != d and not topo.may_write(c, d) and not topo.mates(c, d)]
-        idle = [s for s in cross if not has_mate(cores[s])]
-        pref = idle + [s for s in cross if s not in idle]
-        q = max(0, SW_SHARE - len(same))
-        for i in range(q):
-            straight.add((pref[(i + r) % len(idle)] if q <= len(idle) else pref[i], r))
+    partner = {}
+    for d in cores:
+        m = [e for e in cores if topo.mates(d, e)]
+        partner[d] = m[0] if m else None
+    units = []
+    for d in cores:
+        if not any(d in u for u in units):
+            units.append([d] + ([partner[d]] if partner[d] is not None else []))
+    unit_of = {d: i for i, u in enumerate(units) for d in u}
+    nu = len(units)
+
+    entries = {(u, p): 0 for u in range(nu) for p in (0, 1)}
+    lane, ncross = {}, {}
+    for s, root in enumerate(cores):
+        if partner[root] is not None:
+            for u in range(nu):
+                if u != unit_of[root]:
+                    lane[(s, u)] = plane_of(root)
+                    entries[(u, plane_of(root))] += 1
+    flex = [s for s, root in enumerate(cores) if partner[root] is None]
+    for u in range(nu):
+        fs = [s for s in flex if unit_of[cores[s]] != u]
+        fs = fs[u % len(fs):] + fs[:u % len(fs)]
+        fs.sort(key=lambda s: ncross.get(s, 0))
+        for s in fs:
+            own = plane_of(cores[s])
+            p = own
+            if entries[(u, 1 - own)] < entries[(u, own)] and ncross.get(s, 0) < MAXCROSS:
+                p = 1 - own
+                ncross[s] = ncross.get(s, 0) + 1
+            lane[(s, u)] = p
+            entries[(u, p)] += 1
 
     for s, root in enumerate(cores):
-        chipmates = [c for c in range(WORLD) if c != root and place(c) == place(root)]
-        dests = [(r, d) for r, d in enumerate(cores) if d != root]
+        others = [c for c in on_chip(root) if c != root]
+        over = [x for x in range(WORLD) if topo.mates(x, root)][0]
+        port = [c for c in others if topo.may_write(c, over)]
 
-        def by_turns(cs):
-            a = [c for c in cs if topo.die(c) == topo.die(root)]
-            b = [c for c in cs if topo.die(c) != topo.die(root)]
-            out = []
-            while a or b:
-                if a:
-                    out.append(a.pop(0))
-                if b:
-                    out.append(b.pop(0))
-            return out
+        def deal(cs):
+            a = [c for c in cs if topo.die(c) != topo.die(root)]
+            b = [c for c in cs if topo.die(c) == topo.die(root) and c != root] + [c for c in cs if c == root]
+            return a + b
 
-        def pi(r):
-            return min((2 * s - r) % N, (r - 2 * s) % N)
+        set_a = deal([c for c in others if c not in port] + [root])
+        set_b = deal(port)
+        lone = partner[root] is None
 
-        free_all = by_turns([h for h in chipmates if all(topo.may_write(h, d) for _, d in dests)])
-        helpers = free_all + by_turns([h for h in chipmates if h not in free_all])
-        idx = {h: i for i, h in enumerate(helpers)}
-        k = len(helpers)
+        def gateway(p, gws):
+            cands = [x for x in gws if topo.die(x) == topo.die(set_a[p])]
+            return cands[p % len(cands)]
 
-        targets, covered = [], set()
-        for r, d in dests:
-            if topo.may_write(root, d):
-                continue
-            covered.add(r)
-            if topo.mates(root, d) or (s, r) in straight:
-                targets.append(("X", [(r, d)], [], place(d)))
+        u0 = unit_of[root]
+        targets = []
+        for k in range(1, nu):
+            u = (u0 + k) % nu
+            p = lane[(s, u)]
+            near = [d for d in units[u] if plane_of(d) == p]
+            far = [d for d in units[u] if plane_of(d) != p]
+            cross = p != plane_of(root)
+            if not far:
+                targets.append((cross, [near[0]] * len(PIECES), None, near))
             else:
-                gws = [c for c in range(WORLD) if topo.mates(c, d) and topo.may_write(c, d)]
-                local = [x for x in dests if place(x[1]) == place(gws[0])]
-                covered.update(x[0] for x in local)
-                targets.append(("G", [(r, d)] + local, gws, place(gws[0])))
-        for r, d in dests:
-            if r not in covered:
-                targets.append(("R", [(r, d)], [], place(d)))
+                gws = [c for c in range(WORLD) if topo.mates(c, far[0]) and topo.may_write(c, far[0])]
+                targets.append((cross, [gateway(q, gws) for q in range(len(PIECES))], far[0], near))
 
-        free = {h: k * TPO + (i + 1) * TCO + THOP for i, h in enumerate(helpers)}
-        step = {h: TCF for h in helpers}
-        free[root], step[root] = k * (TPO + TCO), TPF + TCF
-        count = {}
-        busy = has_mate(root)
-        n_x = sum(1 for t in targets if t[0] == "X")
-        slots = []
-        for n, cand in ((n_x, free_all), (len(targets) - n_x, helpers + [root])):
-            for _ in range(n):
-                cc = [c for c in cand if not (busy and c in free_all and count.get(c, 0) >= CAP)] or cand
-                c = min(cc, key=lambda c: free[c] + step[c])
-                free[c] += step[c]
-                count[c] = count.get(c, 0) + 1
-                slots.append((free[c], c))
-        slots.sort()
-
-        left, give = n_x, {}
-        for t in sorted(targets, key=lambda t: (t[0] != "G", min(pi(r) for r, _ in t[1]))):
-            is_x = t[0] == "X"
-            ok = [sl for sl in slots if sl[1] in free_all or not is_x]
-            if not is_x and sum(1 for sl in slots if sl[1] in free_all) <= left:
-                ok = [sl for sl in ok if sl[1] not in free_all]
-            near = [sl for sl in ok if sl[0] <= ok[0][0] + TNEAR]
-            sl = min(near, key=lambda sl: (inload.get((t[3], topo.die(sl[1])), 0), sl[0]))
-            slots.remove(sl)
-            left -= 1 if is_x else 0
-            key = (t[3], topo.die(sl[1]))
-            inload[key] = inload.get(key, 0) + 1
-            give.setdefault(sl[1], []).append((sl[0], t))
-
-        used = [h for h in helpers if h in give]
-        add(0.0, root, "S", s, used)
-        add(0.01, root, "Q", s, used)
-        for c in used + [root]:
-            if c not in give:
-                continue
-            ts0 = TPO * (idx[c] + 1) if c != root else k * (TPO + TCO)
-            tq0 = k * TPO + (idx[c] + 1) * TCO if c != root else k * (TPO + TCO) + 0.01
-            hop = THOP if c != root else 0.0
-            land = []
-            for pos, (tq, t) in enumerate(sorted(give[c], key=lambda x: x[0])):
-                if t[0] == "G":
-                    gw = min([x for x in t[2] if topo.die(x) == topo.die(c)], key=lambda x: gwload.get(x, 0))
-                    gwload[gw] = gwload.get(gw, 0) + 1
-                    land.append(gw)
-                    gwjobs.setdefault(gw, []).append((tq, ts0 + hop + TPF * (pos + 1), s, t[1]))
+        lists = {0: [], 1: []}
+        if lone:
+            quota = (len(targets) + 1) // 2 - sum(1 for t in targets if t[0])
+            turn = 0
+            for t in targets:
+                if t[0]:
+                    lists[1].append(t)
+                elif turn % 2 == 1 and quota > 0:
+                    lists[1].append(t)
+                    quota -= 1
+                    turn += 1
                 else:
-                    land.append(t[1][0][1])
-                    when[(s, t[1][0][0])] = tq
-            add(ts0, c, "S", s, land)
-            add(tq0, c, "Q", s, land)
+                    lists[0].append(t)
+                    turn += 1
+        else:
+            lists[0] = targets
+
+        holders = {q: [] for q in range(len(PIECES))}
+        for q in range(len(PIECES)):
+            if set_a[q] != root:
+                holders[q].append(set_a[q])
+            if lists[1] or not lone:
+                holders[q].append(set_b[q])
+        if not lone:
+            for q in range(len(PIECES)):
+                gwjobs.setdefault(set_b[q], []).append((1.0, s, q, partner[root], []))
+            when[(s, cores.index(partner[root]))] = 2.0
+
+        full = topo.mask(root, others[0])
+        low = off_mask(root, [t[1][PLANE] for t in lists[0]])
+        high = full & ~low
+        call(0.0, root, s, [(0, full, holders[0])])
+        call(0.1, root, s, [(1, low, holders[1]), (2, high, holders[2])])
+        call(0.2, root, s, [(PLANE, high, holders[PLANE]), (PLANE, low, [t[1][PLANE] for t in lists[0]])])
+        for which, senders in ((0, set_a), (1, set_b)):
+            if not lists[which]:
+                continue
+            for q, c in enumerate(senders):
+                lands = [t[1][q] for t in lists[which]]
+                if c != root:
+                    call(1.0, c, s, [(q, off_mask(c, lands), lands)])
+            for pos, t in enumerate(lists[which]):
+                tq = 2.0 + pos
+                if t[2] is None:
+                    when[(s, cores.index(t[3][0]))] = tq
+                else:
+                    for q in range(len(PIECES)):
+                        gwjobs.setdefault(t[1][q], []).append((tq, s, q, t[2], t[3]))
+                    for d in [t[2]] + t[3]:
+                        when[(s, cores.index(d))] = tq + 1.0
 
     for gw, jobs in gwjobs.items():
-        f = 0.0
-        for tq, ts, s, fin in sorted(jobs, key=lambda x: x[0]):
-            add(ts, gw, "S", s, [d for _, d in fin])
-            add(tq, gw, "Q", s, [d for _, d in fin])
-            t = max(f, tq + THOP) + TCF
-            f = t + TPF
-            for r, _ in fin:
-                when[(s, r)] = t
-    ops = {c: [x[1:] for x in sorted(l, key=lambda x: x[0])] for c, l in raw.items()}
+        for tq, s, q, far, near in sorted(jobs, key=lambda x: (x[0], x[1])):
+            m = topo.mask(gw, far)
+            tr = [(q, m, [far])]
+            if near:
+                tr.append((q, topo.mask(gw, near[0]) & ~m, near))
+            call(tq, gw, s, tr)
+    ops = {c: [x[1:] for x in sorted(l, key=lambda x: (x[0], x[1]))] for c, l in raw.items()}
     _CACHE["p"] = (ops, when, arrive)
     return _CACHE["p"]
 
@@ -191,29 +197,29 @@ def rank_program(g, core, T, topo):
         g.vector.quantize_mx(T.Q[:, b:b + CW], T.S[:, b:b + CW], T.cin[:]).then_inc(sem.qz, 1)
         g.vector.wait_ge(sem.ldx, 16)
         g.vector.quantize_mx(T.Q[:, b + CW:b + W], T.S[:, b + CW:b + W], T.xin[:]).then_inc(sem.qz, 1)
-        g.wait_ge(sem.qz, 2)
+
+    def view(s, q):
+        kind, lo, hi = PIECES[q]
+        if kind == "Q":
+            return T.Q[:, s * W + lo:s * W + hi].bitcast(dt.uint8)
+        return T.S[:, s * W + lo:s * W + hi]
 
     sent = 0
-    for kind, s, groups in mine:
-        name = ("aq%d" if kind == "Q" else "as%d") % s
-        if cores[s] != core:
-            g.wait_ge(sem[name], arrive[(core, kind, s)])
-
-        def view():
-            if kind == "Q":
-                return T.Q[:, s * W:(s + 1) * W].bitcast(dt.uint8)
-            return T.S[:, s * W:(s + 1) * W]
-
-        transfers = []
-        for mask, dsts in groups:
+    for s, transfers in mine:
+        if cores[s] == core:
+            g.wait_ge(sem.qz, 1 if all(q == 0 for q, _, _ in transfers) else 2)
+        else:
+            g.wait_ge(sem["a%d" % s], arrive[(core, s)])
+        trs = []
+        for q, mask, dsts in transfers:
             ids = []
             for d in dsts:
                 rid, pid = topo.addr(d, core)
                 ids.append(DstId(rid=rid, pnc=pid))
-            transfers.append(RemoteDMATransfer(dst_ids=ids, dma_engine_mask=mask, remote_sem=sem[name],
-                                               srcs=[view()], dsts=[view() for _ in dsts]))
+            trs.append(RemoteDMATransfer(dst_ids=ids, dma_engine_mask=mask, remote_sem=sem["a%d" % s],
+                                         srcs=[view(s, q)], dsts=[view(s, q) for _ in dsts]))
             sent += _bits(mask)
-        g.remote_dma_fused(transfers, local_sem=sem.sent)
+        g.remote_dma_fused(trs, local_sem=sem.sent)
 
     if rank is not None:
         def ready(j):
@@ -230,8 +236,7 @@ def rank_program(g, core, T, topo):
                 if t == rank:
                     g.tensor.wait_ge(sem.qz, 2)
                 else:
-                    g.tensor.wait_ge(sem["as%d" % t], arrive[(core, "S", t)])
-                    g.tensor.wait_ge(sem["aq%d" % t], arrive[(core, "Q", t)])
+                    g.tensor.wait_ge(sem["a%d" % t], arrive[(core, t)])
             mmx = g.tensor.matmul_mx(T.acc[:, 0:XW],
                                      T.Q[:, kk * W:kk * W + CW], T.S[:, kk * W:kk * W + CW],
                                      T.Q[:, j * W + CW:(j + 1) * W], T.S[:, j * W + CW:(j + 1) * W],

from concourse.bass import DstId, RemoteDMATransfer
from concourse.mybir import dt

N = 16
WORLD = 256
CW, XW = 128, 256
W = CW + XW
PIECES = (("Q", 0, CW), ("Q", CW, CW + XW // 2), ("Q", CW + XW // 2, W), ("S", 0, W))
PLANE = 3
MAXCROSS = 5

SCRATCH = {
    "Q": ("sbuf", [128, N * W], "float8_e4m3fn_x4"),
    "S": ("sbuf", [128, N * W], "uint8"),
    "cin": ("sbuf", [128, 4 * CW], "bfloat16"),
    "xin": ("sbuf", [128, 4 * XW], "bfloat16"),
    "acc": ("psum", [128, 512], "float32"),
    "yout": ("sbuf", [128, XW], "float32"),
}
SEMAPHORES = ["a%d" % s for s in range(N)] + ["ldc", "ldx", "qz", "sent", "mm", "cp", "st"]

_CACHE = {}


def _bits(mask):
    return bin(mask).count("1")


def _plan(cores, topo):
    if "p" in _CACHE:
        return _CACHE["p"]
    raw, when, arrive, gwjobs = {}, {}, {}, {}

    def place(c):
        return (topo.host(c), topo.chip(c))

    def on_chip(c):
        return [x for x in range(WORLD) if place(x) == place(c)]

    def plane_of(c):
        return 0 if place(c) == place(cores[0]) or topo.same_plane(c, cores[0]) else 1

    def call(t, core, s, transfers):
        for _, m, ds in transfers:
            for d in ds:
                arrive[(d, s)] = arrive.get((d, s), 0) + _bits(m)
        raw.setdefault(core, []).append((t, s, transfers))

    def off_mask(c, ds):
        m = topo.mask(c, ds[0])
        for d in ds:
            m &= topo.mask(c, d)
        return m

    partner = {}
    for d in cores:
        m = [e for e in cores if topo.mates(d, e)]
        partner[d] = m[0] if m else None
    units = []
    for d in cores:
        if not any(d in u for u in units):
            units.append([d] + ([partner[d]] if partner[d] is not None else []))
    unit_of = {d: i for i, u in enumerate(units) for d in u}
    nu = len(units)

    entries = {(u, p): 0 for u in range(nu) for p in (0, 1)}
    lane, ncross = {}, {}
    for s, root in enumerate(cores):
        if partner[root] is not None:
            for u in range(nu):
                if u != unit_of[root]:
                    lane[(s, u)] = plane_of(root)
                    entries[(u, plane_of(root))] += 1
    flex = [s for s, root in enumerate(cores) if partner[root] is None]
    for u in range(nu):
        fs = [s for s in flex if unit_of[cores[s]] != u]
        fs = fs[u % len(fs):] + fs[:u % len(fs)]
        fs.sort(key=lambda s: ncross.get(s, 0))
        for s in fs:
            own = plane_of(cores[s])
            p = own
            if entries[(u, 1 - own)] < entries[(u, own)] and ncross.get(s, 0) < MAXCROSS:
                p = 1 - own
                ncross[s] = ncross.get(s, 0) + 1
            lane[(s, u)] = p
            entries[(u, p)] += 1

    for s, root in enumerate(cores):
        others = [c for c in on_chip(root) if c != root]
        over = [x for x in range(WORLD) if topo.mates(x, root)][0]
        port = [c for c in others if topo.may_write(c, over)]

        def deal(cs):
            a = [c for c in cs if topo.die(c) != topo.die(root)]
            b = [c for c in cs if topo.die(c) == topo.die(root) and c != root] + [c for c in cs if c == root]
            return a + b

        set_a = deal([c for c in others if c not in port] + [root])
        set_b = deal(port)
        lone = partner[root] is None

        def gateway(p, gws):
            cands = [x for x in gws if topo.die(x) == topo.die(set_a[p])]
            return cands[p % len(cands)]

        u0 = unit_of[root]
        targets = []
        for k in range(1, nu):
            u = (u0 + k) % nu
            p = lane[(s, u)]
            near = [d for d in units[u] if plane_of(d) == p]
            far = [d for d in units[u] if plane_of(d) != p]
            cross = p != plane_of(root)
            if not far:
                targets.append((cross, [near[0]] * len(PIECES), None, near))
            else:
                gws = [c for c in range(WORLD) if topo.mates(c, far[0]) and topo.may_write(c, far[0])]
                targets.append((cross, [gateway(q, gws) for q in range(len(PIECES))], far[0], near))

        lists = {0: [], 1: []}
        if lone:
            quota = (len(targets) + 1) // 2 - sum(1 for t in targets if t[0])
            turn = 0
            for t in targets:
                if t[0]:
                    lists[1].append(t)
                elif turn % 2 == 1 and quota > 0:
                    lists[1].append(t)
                    quota -= 1
                    turn += 1
                else:
                    lists[0].append(t)
                    turn += 1
        else:
            lists[0] = targets

        holders = {q: [] for q in range(len(PIECES))}
        for q in range(len(PIECES)):
            if set_a[q] != root:
                holders[q].append(set_a[q])
            if lists[1] or not lone:
                holders[q].append(set_b[q])
        if not lone:
            for q in range(len(PIECES)):
                gwjobs.setdefault(set_b[q], []).append((1.0, s, q, partner[root], []))
            when[(s, cores.index(partner[root]))] = 2.0

        full = topo.mask(root, others[0])
        low = off_mask(root, [t[1][PLANE] for t in lists[0]])
        high = full & ~low
        call(0.0, root, s, [(0, full, holders[0])])
        call(0.1, root, s, [(1, low, holders[1]), (2, high, holders[2])])
        call(0.2, root, s, [(PLANE, high, holders[PLANE]), (PLANE, low, [t[1][PLANE] for t in lists[0]])])
        for which, senders in ((0, set_a), (1, set_b)):
            if not lists[which]:
                continue
            for q, c in enumerate(senders):
                lands = [t[1][q] for t in lists[which]]
                if c != root:
                    call(1.0, c, s, [(q, off_mask(c, lands), lands)])
            for pos, t in enumerate(lists[which]):
                tq = 2.0 + pos
                if t[2] is None:
                    when[(s, cores.index(t[3][0]))] = tq
                else:
                    for q in range(len(PIECES)):
                        gwjobs.setdefault(t[1][q], []).append((tq, s, q, t[2], t[3]))
                    for d in [t[2]] + t[3]:
                        when[(s, cores.index(d))] = tq + 1.0

    for gw, jobs in gwjobs.items():
        for tq, s, q, far, near in sorted(jobs, key=lambda x: (x[0], x[1])):
            m = topo.mask(gw, far)
            tr = [(q, m, [far])]
            if near:
                tr.append((q, topo.mask(gw, near[0]) & ~m, near))
            call(tq, gw, s, tr)
    ops = {c: [x[1:] for x in sorted(l, key=lambda x: (x[0], x[1]))] for c, l in raw.items()}
    _CACHE["p"] = (ops, when, arrive)
    return _CACHE["p"]


def rank_program(g, core, T, topo):
    cores = list(T.cores)
    ops, when, arrive = _plan(cores, topo)
    rank = T.rank_of(core)
    mine = ops.get(core, [])
    if rank is None and not mine:
        return
    sem = T.sem

    if rank is not None:
        b = rank * W
        g.sync.dma_start(T.cin[:], T.c[:]).then_inc(sem.ldc, 16)
        g.scalar.dma_start(T.xin[:], T.x[:]).then_inc(sem.ldx, 16)
        g.vector.wait_ge(sem.ldc, 16)
        g.vector.quantize_mx(T.Q[:, b:b + CW], T.S[:, b:b + CW], T.cin[:]).then_inc(sem.qz, 1)
        g.vector.wait_ge(sem.ldx, 16)
        g.vector.quantize_mx(T.Q[:, b + CW:b + W], T.S[:, b + CW:b + W], T.xin[:]).then_inc(sem.qz, 1)

    def view(s, q):
        kind, lo, hi = PIECES[q]
        if kind == "Q":
            return T.Q[:, s * W + lo:s * W + hi].bitcast(dt.uint8)
        return T.S[:, s * W + lo:s * W + hi]

    sent = 0
    for s, transfers in mine:
        if cores[s] == core:
            g.wait_ge(sem.qz, 1 if all(q == 0 for q, _, _ in transfers) else 2)
        else:
            g.wait_ge(sem["a%d" % s], arrive[(core, s)])
        trs = []
        for q, mask, dsts in transfers:
            ids = []
            for d in dsts:
                rid, pid = topo.addr(d, core)
                ids.append(DstId(rid=rid, pnc=pid))
            trs.append(RemoteDMATransfer(dst_ids=ids, dma_engine_mask=mask, remote_sem=sem["a%d" % s],
                                         srcs=[view(s, q)], dsts=[view(s, q) for _ in dsts]))
            sent += _bits(mask)
        g.remote_dma_fused(trs, local_sem=sem.sent)

    if rank is not None:
        def ready(j):
            return max(when.get((j, rank), 0.0), when.get(((rank - j) % N, rank), 0.0))

        order = sorted(range(N), key=lambda j: (ready(j), j))
        seen = set()
        for i, j in enumerate(order):
            kk = (rank - j) % N
            for t in (j, kk):
                if t in seen:
                    continue
                seen.add(t)
                if t == rank:
                    g.tensor.wait_ge(sem.qz, 2)
                else:
                    g.tensor.wait_ge(sem["a%d" % t], arrive[(core, t)])
            mmx = g.tensor.matmul_mx(T.acc[:, 0:XW],
                                     T.Q[:, kk * W:kk * W + CW], T.S[:, kk * W:kk * W + CW],
                                     T.Q[:, j * W + CW:(j + 1) * W], T.S[:, j * W + CW:(j + 1) * W],
                                     i == 0, i == N - 1)
            if i == N - 1:
                mmx.then_inc(sem.mm, 1)
        g.vector.wait_ge(sem.mm, 1)
        g.vector.tensor_copy(T.yout[:], T.acc[:, 0:XW]).then_inc(sem.cp, 1)
        g.sync.wait_ge(sem.cp, 1)
        g.sync.dma_start(T.y[:], T.yout[:]).then_inc(sem.st, 16)
        g.sync.wait_ge(sem.st, 16)

    if sent:
        g.wait_ge(sem.sent, sent)
